import numpy as np, ml_dtypes
CORES = [3,11,19,27,35,43]
N = 6
BF = ml_dtypes.bfloat16
P, V, C, PH, S, Z, CAP, RO = 3072, 1152, 512, 3, 8, 8, 96, 4
I = V // PH
def tail(rng, b, top):
    return np.where(np.arange(16)[:, None] >= rng.integers(0, 17, (N, 8, 1, V)), rng.integers(0, top, b.shape), b)
def parts(rng):
    e = rng.choice(np.array([10.0, 14.0, 18.0, 24.0]), (N, 8, 1, 1))
    x = np.minimum((256 * rng.random((N, 8, 16, P)) ** e).astype(np.int64), 255)
    m = rng.integers(0, 256, (N, 8, 16, V)); b = rng.integers(0, P, (N, 8, 16, V))
    return x, m, b, tail(rng, b, P), rng.integers(0, V, (N, 8, 16, C))
def tops(x, l):
    y = np.take_along_axis(x, l[:, :, 0][:, :, None, :], 3)
    for k in range(1, 16): y = np.maximum(y, np.take_along_axis(x, l[:, :, k][:, :, None, :], 3))
    return y
def late(rng, shape):
    return PH * rng.integers(0, I, shape) + 1 + rng.integers(0, PH - 1, shape)
def pack(x, m, b, d, u):
    r = {"mor": x.reshape(N, 128, P).astype(np.float32).astype(BF), "mea": m.reshape(N, 128, V).astype(np.float32).astype(BF)}
    r["bas"] = b.reshape(N, 128, V).astype(np.int32); r["der"] = d.reshape(N, 128, V).astype(np.int32); r["use"] = u.reshape(N, 128, C).astype(np.int32)
    return r
def setup_inputs(rng):
    x, m, b, d, u = parts(rng); h = rng.integers(0, 8, N)
    for q in range(N):
        g = int(h[q]); x[q, g, :, P - 1] = 255; m[q, g] = rng.integers(0, 151, (16, V)); u[q, g] = late(rng, (16, C))
        d[q, g, rng.integers(0, 16, I), PH * np.arange(I)] = P - 1
    near = rng.random((N, 8, 1, V)) < rng.choice(np.array([0.0, 0.2, 0.5, 0.8]), (N, 8, 1, 1)); near[np.arange(N), h] = False
    m = np.where(near, np.clip(tops(x, d) + rng.integers(-24, 25, m.shape), 0, 255), m)
    for q in range(N):
        for g in range(8):
            v = PH * rng.permutation(I)[:3]; u[q, g][:, b[q, g, 15, v] & (C - 1)] = v
    return pack(x, m, b, d, u)
def setup_inputs_corners(rng):
    x, m, b, d, u = parts(rng); x = np.minimum(x, 100); x[..., P - 1] = 255; m = rng.integers(0, 101, m.shape)
    b = rng.integers(0, P - 1, b.shape); d = tail(rng, b, P - 1); u = late(rng, u.shape)
    u = np.where(rng.random((N, 8, 1, C)) < 0.1, np.where(rng.random((N, 8, 1, C)) < 0.5, V - 1, 1), u); top = tops(x, d)
    for q in range(N):
        for g in range(8):
            if q == 3 and g % 2 == 1:
                n = (0, 1, CAP // 2, CAP - 1)[g // 2]; o = PH * np.arange(I); w = PH * rng.permutation(I) + 1
                m[q, g][:, o] = top[q, g][:, o]; m[q, g][:, w[:n]] = top[q, g][:, w[:n]]
                d[q, g, rng.integers(0, 16, I - n), w[n:]] = P - 1; u[q, g] = PH * rng.integers(0, I, (16, C))
                continue
            n = int(rng.choice(np.array([0, 1, CAP - 1, CAP, CAP + 1, I])))
            if q == 0: n = (CAP, CAP + 1, I, CAP - 1, 1, 0, CAP, CAP + 1)[g]
            if q == 1 or q == 2: n = (CAP, 1, CAP - 1, 0)[g % 4]
            if q == 2 and g == 7: n = CAP + 1
            o = PH * rng.permutation(I); nl = min(n, C // 2); lone, fit, ad = o[:nl], o[nl:n], o[n:]
            cols = 2 * rng.permutation(C // 2)[:nl] + q % 2
            b[q, g, 15, lone] = cols + C * rng.integers(0, P // C - 1, nl); u[q, g][:, cols] = lone
            b[q, g, 15, ad] = 2 * rng.integers(0, C // 2, I - n) + 1 - q % 2 + C * rng.integers(0, P // C - 1, I - n)
            bad = np.concatenate([lone, ad]); d[q, g, rng.integers(0, 16, len(bad)), bad] = P - 1
            m[q, g][:, fit] = top[q, g][:, fit]
            if q == 2:
                o = PH * np.arange(I); z = np.add.reduce(np.arange(1, 17)[:, None] * m[q, g][:, o], axis=0) & (Z - 1)
                left = np.ones(P, dtype=bool); left[P - 1] = False; left[S * np.arange(I) + z] = False
                l = d[q, g][:, o + 1]; l = np.where(left[l], l, rng.choice(np.flatnonzero(left), l.shape))
                d[q, g][:, o + 1] = l; m[q, g][:, o + 1] = np.maximum.reduce(x[q, g][:, l], axis=1)
    return pack(x, m, b, d, u)
def setup_inputs_ties(rng):
    x, m, b, d, u = parts(rng); x[:, 1::2] = x[:, 1::2] >> 6
    k = rng.integers(0, 8, (N, 8, 1, V)); m = np.take_along_axis(m[..., :8], k, 3); m[:, 1::2] = m[:, 1::2] >> 6
    b[:, :2] = np.take_along_axis(b[:, :2, :, :8], k[:, :2], 3); d[:, :2] = np.take_along_axis(d[:, :2, :, :8], k[:, :2], 3)
    lane = np.arange(V); a = rng.integers(40, 81, (N, 16, 1)); high = (np.arange(16)[:, None] == 15) & (lane >= V // 2)
    m[:, 6] = np.where(lane % PH == 0, rng.integers(215, 256, (N, 16, V)), a + high); u[:, 6] = late(rng, (N, 16, C))
    u[..., ::2] = u[:, :, np.arange(16) & 3, ::2]
    return pack(x, m, b, d, u)
def setup_inputs_alike(rng):
    x, m, b, d, u = parts(rng)
    d[:, :3] = b[:, :3]; d[:, 1, 0] = (b[:, 1, 0] + 1) % P; d[:, 2, 15] = (b[:, 2, 15] + 1) % P
    b[:, 3, 15] = rng.integers(0, P, (N, 1)); u[:, 4] = rng.integers(0, V, (N, 1, C))
    for q in range(N):
        v = PH * rng.permutation(I)[:I // 4]; u[q, 4][:, b[q, 4, 15, v] & (C - 1)] = v
    b[:, 5] = rng.integers(0, P, (N, 1, V)); d[:, 5] = rng.integers(0, P, (N, 1, V)); u[:, 6] = (V - 1) * rng.integers(0, 2, (N, 16, C))
    for q in range(N):
        v = PH * rng.permutation(I)[:I // 8]; c = b[q, 7, 15, v] & (C - 1); u[q, 7][:, c] = v; u[(q + 1) % N, 7][:, c] = v
    return pack(x, m, b, d, u)
def setup_inputs_spread(rng):
    x = (np.exp2(8 * rng.random((N, 8, 1, P))) * rng.random((N, 8, 16, P)) ** 3).astype(np.int64)
    m = (np.exp2(8 * rng.random((N, 8, 1, V))) * rng.random((N, 8, 16, V))).astype(np.int64)
    e = rng.choice(np.array([1.0, 2.0, 4.0, 8.0]), (3, N, 8, 1, 1))
    b = (P * rng.random((N, 8, 16, V)) ** e[0]).astype(np.int64); c = (P * rng.random((N, 8, 16, V)) ** e[1]).astype(np.int64)
    d = np.where(np.arange(16)[:, None] >= rng.integers(0, 17, (N, 8, 1, V)), c, b); u = (V * rng.random((N, 8, 16, C)) ** e[2]).astype(np.int64)
    return pack(np.clip(x, 0, 255), np.clip(m, 0, 255), np.clip(b, 0, P - 1), np.clip(d, 0, P - 1), np.clip(u, 0, V - 1))
def setup_inputs_ends(rng):
    def bits(p, n): return 255 * (rng.random((N, 8, 16, n)) < p)
    def lists(n, hi):
        k = rng.random((N, 8, 1, n)); a = hi * rng.integers(0, 2, (N, 8, 16, n))
        return np.where(k < 0.25, 0, np.where(k < 0.5, hi, np.where(k < 0.8, a, rng.integers(0, hi + 1, (N, 8, 16, n)))))
    k = rng.random((N, 8, 1, P)); x = np.where(k < 0.6, 0, np.where(k < 0.63, 255, bits(0.06, P)))
    k = rng.random((N, 8, 1, V)); m = np.where(k < 0.25, 0, np.where(k < 0.5, 255, bits(0.5, V)))
    b = lists(V, P - 1); d = np.where(np.arange(16)[:, None] >= rng.integers(0, 17, (N, 8, 1, V)), lists(V, P - 1), b); u = lists(C, V - 1)
    for t in range(RO):
        for c in (97 * t, 97 * t - 1):
            u[..., c & (C - 1)] = np.where(rng.random((N, 8, 16)) < 0.5, (V - 1) * rng.integers(0, 2, (N, 8, 16)), rng.integers(0, V, (N, 8, 16)))
    x[:, ::2, :, 0] = 255 * rng.integers(0, 2, (N, 4, 16)); x[:, ::2, :, P - 1] = 255 * rng.integers(0, 2, (N, 4, 16)); x[:, 1::2, :, 0] = 0; x[:, 1::2, :, P - 1] = 255
    lo, hi = PH - 1 + PH * (PH % 2), V - 1 - PH
    m[:, 1::2, :, :PH - 1] = 0; m[:, 1::2, :, V - PH:V - 1] = 255; m[..., V - 1] = 255
    m[:, 1::2, :, lo] = 0; m[:, 1::2, :, hi] = 0; m[:, ::2, :, lo] = 255; m[:, ::2, :, hi] = 255
    u[:, 1::2, :, 0] = np.where(np.arange(16) % 2 == 0, 0, V - 1); b[:, 1::2, :, 0] = 0; d[:, 1::2, :, 0] = P - 1
    u[..., C - 1] = np.where(np.arange(16) % 2 == 0, hi, lo)
    b[..., lo] = 0; d[..., lo] = P - 1; b[..., hi] = P - 1; d[..., hi] = 0; d[..., V - 1] = 0
    b[:, :, 15, V - 1] = ((C - 1 - 97 * (PH - 1)) & (C - 1)) + P - C
    return pack(x, m, b, d, u)
def check_inputs(d):
    bad = []
    for k, hi in (("mor", 255), ("mea", 255), ("bas", P - 1), ("der", P - 1), ("use", V - 1)):
        a = np.asarray(d[k]).astype(np.float64)
        if not np.all((a >= 0) & (a <= hi) & (a == np.floor(a))): bad.append("range of " + k)
    return bad
def pick(a, ix):
    return np.stack([np.take(a[g], ix[g], axis=1) for g in range(8)])
def model(kap, mv, own, m, b, d, u):
    c = pick(u, kap)
    s = np.add.reduce(np.abs(pick(m, c) - mv[:, :, None, :]), axis=1)
    k = np.minimum.reduce(np.where(c == own, 2 ** 24, s * 2048 + c), axis=1)
    ok = k < 2 ** 24; w = np.where(ok, k & 2047, 0); dm = pick(d, w)
    diff = pick(b, w) != dm; diff[:, 15] = True
    return ok, w, np.argmax(diff, axis=1), dm
def gap(x, l, mv):
    return np.add.reduce(np.abs(np.maximum.reduce(pick(x, l), axis=2) - mv), axis=1)
def reference(mor, mea, bas, der, use):
    x = mor.astype(np.float32).astype(np.int32).reshape(N, 8, 16, P); m = mea.astype(np.float32).astype(np.int32).reshape(N, 8, 16, V)
    b = bas.astype(np.int32).reshape(N, 8, 16, V); d = der.astype(np.int32).reshape(N, 8, 16, V); u = use.astype(np.int32).reshape(N, 8, 16, C)
    row = np.arange(16)[None, :, None]; i = np.arange(I); count = [0] * N
    for t in range(RO):
        v = PH * i + t % PH; todo = []
        for r in range(N):
            mv = m[r][:, :, v]; bv = b[r][:, :, v]; dv = d[r][:, :, v]; kap = (bv[:, 15] + 97 * t) & (C - 1); mar = count[r] & 127
            ok, w, f, dm = model(kap, mv, v, m[r], b[r], d[r], u[r])
            e = np.where(row < f[:, None, :], bv, dm); old = gap(x[r], dv, mv)
            ad = ok & (gap(x[r], e, mv) + mar < old)
            q = (r + 1 + t % (N - 1)) % N
            sel = np.argsort(ad, axis=1, kind="stable")[:, :CAP]
            asks = ~np.take_along_axis(ad, sel, 1); mv2 = pick(mv, sel)
            ok2, w2, f2, dm2 = model(np.take_along_axis(kap, sel, 1), mv2, -1, m[q], b[q], d[q], u[q])
            e2 = np.where(row < f2[:, None, :], pick(bv, sel), dm2)
            ad2 = asks & (gap(x[r], e2, mv2) + mar < np.take_along_axis(old, sel, 1))
            new = np.where(ad[:, None, :], e, dv); got = ad.copy()
            for g in range(8):
                new[g][:, sel[g][ad2[g]]] = e2[g][:, ad2[g]]; got[g, sel[g][ad2[g]]] = True
            todo.append((ad, w, new, got, (np.add.reduce((row + 1) * mv, axis=1) + t) & (Z - 1)))
        for r in range(N):
            ad, w, new, got, z = todo[r]; d[r][:, :, v] = new; count[r] = int(np.count_nonzero(got))
            for g in range(8):
                j = i[ad[g]]; u[r, g, (j + t) & 15, (j + 37 * t) & (C - 1)] = w[g][j] ^ 1
                j = i[got[g]]; x[r, g][:, S * j + z[g][j]] = m[r, g][:, v[j]]
    return {"yd": d.reshape(N, 128, V).astype(np.float32), "yu": u.reshape(N, 128, C).astype(np.float32), "ym": x.reshape(N, 128, P).astype(np.float32).astype(BF)}

from concourse.mybir import AluOpType as OP, ActivationFunctionType as AF

NR = 6
P, V, C, PH, I, CAP, RO = 3072, 1152, 512, 3, 384, 96, 4
IX = I + CAP
VX = V + PH * CAP
W16 = 16 * I
CH = 96
SC = 128
VC, NVC = 64, 4
EV = [0, 3, 3, 3]
BIG = float(1 << 23)
FIRST = "cvdewvfwvhwivwspq"
ORDER = "bacadvawevfavwhviawaw"

SCRATCH = {}


def _sb(dtype, **kw):
    for n, w in kw.items():
        SCRATCH[n] = ("sbuf", [128, w], dtype)


_sb("int32", bas_i=V, der_i=V, use_i=C, pi=8, clsi=96, zi=96, mi=24, ni=8, KUg=I, U=I, Ea=IX, nmi=8, KQs=CAP, uq=CAP, E2=CAP)
_sb("uint16", cls=96, zof=96, use16=C, u16=I, d16=I, e16=I, m16=24, s16=8, sv16=8, n16=8, uq16=CAP, e216=CAP)
_sb("float32", Bf=VX, Dv=V, W=V, KU=C, KLX=V, VR=V, onef=144, selr=144, swp=512, oall=128, pm=8, pw=8, cb=8, i8=96, dgf=400,
    amask=I, acc=8, KEY=I, KT=I, KS=I, thr=IX, nm=8, cnt=8, KN=I, KQ=IX, KEY2=CAP, KT2=CAP, KS2=CAP, Bs=CAP, ths=CAP)
_sb("bfloat16", meas=VX, morph=P, oneb=I, sel1=144, selm=144, selp=144, selq=144, selz=144, blk=128, blkn=128, blk2=128,
    blk2n=128, tri=128, cst=128, idb=128, idn=128, idbig=128, blkK=128, dg=400, rmask=16 * SC, c128=IX, Z=16 * SC,
    GM=16 * SC, RA=16 * SC, EQ=I, GD=W16, GE=W16, SD=W16, SE=W16, MD=I, ME=I, got=IX, non=IX, cum=IX, junk=IX, old=I, gx=I,
    NEQ=V, GQ=16 * CAP, RQ=16 * CAP, S2=16 * CAP, MM2=CAP, ad2=CAP, x0=16 * VC * NVC, x1=16 * VC * NVC, x2=16 * VC * NVC)
for _t in range(RO):
    _sb("bfloat16", **{"qm%d" % _t: V})
    _sb("float32", **{"qk%d" % _t: C, "qw%d" % _t: V})
for _t in range(8):
    SCRATCH["P%d" % _t] = ("psum", [128, 512], "float32")
SEMAPHORES = ["q_v", "q_a", "q_t", "q_g"] + ["d%d" % k for k in range(9)] + ["l%d" % k for k in range(12)] + ["r%s%d" % (a, k) for a in "mkw" for k in range(RO)]


def R(name, lo=0, hi=None, step=1):
    return (name, lo, SCRATCH[name][1][1] if hi is None else hi, step)


def make(g, T):
    eng = {"v": g.vector, "a": g.scalar, "t": g.tensor, "g": g, "s": g.sync}
    count, known, waited, hist, total = {}, {k: {} for k in eng}, {}, {}, {}

    def ap(r):
        if r[0] == "@":
            return ap(r[1]).indirect(ap(r[2]))
        n, lo, hi, st = r
        return T[n][:, lo:hi] if st == 1 else T[n][:, lo:hi:st]

    def acc(reads, writes):
        a = []
        for w, rs in ((0, reads), (1, writes)):
            for r in rs:
                if r[0] == "@":
                    a += [(r[1], w), (r[2], 0)]
                else:
                    a.append((r, w))
        return a

    def sync(q, accs):
        need = []
        for (n, lo, hi, st), w in accs:
            ps = SCRATCH[n][0] == "psum"
            for e in hist.get(n, []):
                if ps and q == "t" and e[3] == "t":
                    continue
                if (ps and e[3] != q) or ((w or e[2]) and lo < e[1] and e[0] < hi):
                    need.append(e)
        need.sort(key=lambda e: -e[5])
        k = known[q]
        for e in need:
            if k.get(e[4], 0) >= e[5]:
                continue
            eng[q].wait_ge(T.sem[e[4]], e[5])
            waited[e[4]] = max(waited.get(e[4], 0), e[5])
            for s, v in e[6].items():
                k[s] = max(k.get(s, 0), v)
            k[e[4]] = max(k.get(e[4], 0), e[5])

    def note(q, accs, sem, val):
        clock = dict(known[q]) if q in known else {}
        for (n, lo, hi, st), w in accs:
            ps = SCRATCH[n][0] == "psum"
            keep = []
            for e in hist.get(n, []):
                same = e[0] == lo and e[1] == hi and e[7] == st
                if ps and e[3] != q:
                    continue
                if w and (same or (st == 1 and lo <= e[0] and e[1] <= hi)):
                    continue
                if not w and not e[2] and same and e[3] == q and e[4] == sem:
                    continue
                keep.append(e)
            keep.append((lo, hi, w, q, sem, val, clock, st))
            hist[n] = keep

    def do(q, reads, writes, call):
        a = acc(reads, writes)
        sync(q, a)
        s = "q_" + q
        count[q] = total[s] = count.get(q, 0) + 1
        call().then_inc(T.sem[s], 1)
        note(q, a, s, count[q])

    def isr(x):
        return isinstance(x, tuple)

    def tt(out, a, b, op):
        do("v", [a, b], [out], lambda: g.vector.tensor_tensor(out=ap(out), in0=ap(a), in1=ap(b), op=op))

    def ts(out, a, s1, s2, op0, op1=None):
        rs = [a] + [s for s in (s1, s2) if isr(s)]
        v = [ap(s) if isr(s) else s for s in (s1, s2)]
        kw = {} if op1 is None else {"op1": op1}
        do("v", rs, [out], lambda: g.vector.tensor_scalar(out=ap(out), in0=ap(a), scalar1=v[0], scalar2=v[1], op0=op0, **kw))

    def cp(out, a):
        do("v", [a], [out], lambda: g.vector.tensor_copy(out=ap(out), in_=ap(a)))

    def ms(out, c):
        do("v", [], [out], lambda: g.vector.memset(ap(out), c))

    def scan(out, a, b, op0, op1):
        do("v", [a, b], [out], lambda: g.vector.tensor_tensor_scan(out=ap(out), data0=ap(a), data1=ap(b), initial=0.0, op0=op0, op1=op1))

    def tr(out, a):
        do("v", [a], [out], lambda: g.vector.transpose(out=ap(out), in_=ap(a)))

    def act(out, a, func=AF.Copy, bias=None, accum=None):
        kw = {}
        if bias is not None:
            kw["bias"] = ap(bias)
        if accum is not None:
            kw["accum_out"] = ap(accum)
        do("a", [a] + [b for b in [bias] if b], [out] + [b for b in [accum] if b],
           lambda: g.scalar.activation(out=ap(out), in_=ap(a), func=func, **kw))

    def mm(out, lhsT, rhs, start, stop):
        do("t", [lhsT, rhs], [out], lambda: g.tensor.matmul(ap(out), ap(lhsT), ap(rhs), start, stop))

    def iota(out, pattern, base, cm):
        kw = {} if SCRATCH[out[0]][2] == "int32" else {"allow_small_or_imprecise_dtypes": True}
        do("g", [], [out], lambda: g.iota(ap(out), pattern, base, cm, **kw))

    def aff(out, a, pattern, op, base, cm):
        do("g", [a], [out], lambda: g.affine_select(ap(out), ap(a), pattern, op, 0.0, base, cm))

    nd, nl = [0], [0]

    def dma(q, out, a):
        accs = acc([a] if isr(a) else [], [out] if isr(out) else [])
        sync(q, accs)
        s = "d%d" % nd[0]
        nd[0] += 1
        total[s] = 16
        eng[q].dma_start(out=ap(out) if isr(out) else out, in_=ap(a) if isr(a) else a).then_inc(T.sem[s], 16)
        note("dma" + s, accs, s, 16)

    def send(topo, src, dst, land, a, rsem):
        accs = acc([a], [])
        sync("g", accs)
        s = "l%d" % nl[0]
        nl[0] += 1
        rid, pid, _ = topo.addr(dst)
        total[s] = len(topo.engines(src, dst))
        g.remote_dma(out_ap=T[land][:], in_ap=ap(a), remote_sem=T.sem[rsem], local_sem=T.sem[s], pid=pid, routing_id=rid, dma_engine_mask=topo.mask(src, dst))
        note("rem" + s, accs, s, total[s])

    def arrive(land, rsem, n):
        total[rsem] = n
        note("arr" + rsem, acc([], [R(land)]), rsem, n)

    def finish():
        for s, n in total.items():
            if waited.get(s, 0) < n:
                g.wait_ge(T.sem[s], n)

    return {"tt": tt, "ts": ts, "cp": cp, "ms": ms, "scan": scan, "tr": tr, "act": act, "mm": mm, "iota": iota, "aff": aff,
            "dma": dma, "send": send, "arrive": arrive, "finish": finish}


def rank_program(g, core, T, topo):
    rank = T.rank_of(core)
    if rank is None:
        return
    F = make(g, T)
    tt, ts, cp, ms, scan, tr, act, mm = (F[k] for k in ("tt", "ts", "cp", "ms", "scan", "tr", "act", "mm"))
    iota, aff, dma, send, arrive = (F[k] for k in ("iota", "aff", "dma", "send", "arrive"))
    asker = [T.cores[(rank - 1 - t) % NR] for t in range(RO)]
    asked = [T.cores[(rank + 1 + t) % NR] for t in range(RO)]
    for t in range(RO):
        for a in "mkw":
            arrive("q%s%d" % (a, t), "r%s%d" % (a, t), len(topo.engines(asked[t], core)))

    def at(win, off):
        return ("@", win, off)

    def col(n, k=0):
        return R(n, k, k + 1)

    def lanes(n, ph):
        return R(n, ph, V, PH)

    def ch(n, k, w):
        return R(n, w * k, w * (k + 1))

    def sk(name, k):
        return R(name, 15 - k, 15 - k + 128)

    def cls(t):
        return ch("cls", t, 24)

    def zof(t):
        return ch("zof", t, 24)

    MO, MS = R("morph"), R("meas", 0, V)

    dma("s", R("bas_i"), T.bas[:])
    dma("a", MS, T.mea[:])
    dma("s", R("use_i"), T.use[:])
    dma("s", R("der_i"), T.der[:])
    dma("s", MO, T.mor[:])

    ms(R("onef"), 1.0)
    aff(R("selr"), R("onef"), [[1, 144]], OP.is_equal, 0, -1)
    aff(R("selr"), R("selr"), [[0, 9], [1, 16]], OP.is_equal, -15, 0)
    ms(R("oneb"), 1.0)
    aff(R("sel1"), R("oneb", 0, 144), [[0, 9], [1, 16]], OP.is_equal, -15, 0)
    aff(R("sel1"), R("sel1"), [[-16, 9], [0, 16]], OP.is_ge, 0, 1)
    aff(R("sel1"), R("sel1"), [[16, 9], [0, 16]], OP.is_ge, 15, -1)
    iota(R("pi", 0, 1), [[0, 1]], 0, 1)
    iota(R("i8"), [[0, 4], [128, 24]], 0, 0)
    iota(R("cb", 0, 6), [[-16, 6]], 0, 0)
    aff(R("idb"), R("oneb", 0, 128), [[1, 128]], OP.is_equal, 0, -1)
    aff(R("blk"), R("oneb", 0, 128), [[-16, 8], [0, 16]], OP.is_ge, 0, 1)
    aff(R("blk"), R("blk"), [[16, 8], [0, 16]], OP.is_ge, 15, -1)
    aff(R("tri"), R("blk"), [[1, 128]], OP.is_ge, 0, -1)
    iota(R("VR"), [[1, V]], 0, 0)
    for h in range(2):
        for y in range(2):
            o = ch("swp", 2 * h + y, 128)
            aff(o, R("onef", 0, 128), [[1, 128]], OP.is_equal, -16 * (h - y), -1)
            aff(o, o, [[0, 4], [1, 2], [0, 16]], OP.is_equal, -h, 0)
    iota(R("dgf"), [[0, 25], [1, 16]], 0, 0)
    iota(R("KLX"), [[2, V // 2], [-1, 2]], 1, 0)
    ms(R("rmask"), 1.0)
    ms(R("rmask", 0, 16 * SC, 16), 0.0)
    ms(R("Z"), 0.0)
    ms(R("amask"), -2.0 * 2 ** 25)
    ms(R("amask", 0, I, 16), 2.0 * 2 ** 25)
    ms(R("Bf", V, VX), 0.0)
    ms(R("meas", V, VX), 0.0)
    ms(R("cst"), -32.0)
    ms(R("cst", 15, 128, 16), 32.0)
    ms(R("nm", 0, 1), 0.0)
    ms(R("thr", I, IX), -1e9)
    ms(R("non", I, IX), 1.0)
    ms(R("c128"), 128.0)
    ms(R("KQ", I, IX), 0.0)
    ms(R("Ea", I, IX), 0)
    ms(R("got", I, IX), 0.0)
    ms(R("oall"), 0.0625)

    def classes(rounds, ph):
        for t in rounds:
            c = ch("clsi", t, 24)
            ts(c, ch("P2", ph, 24), float(97 * t), None, OP.add)
            ts(c, c, 511, None, OP.bitwise_and)
            cp(cls(t), c)

    def class_rows(ph):
        for x in range(16):
            mm(ch("P2", ph, 24), sk("selr", x), R("Bf", 3 * x + ph, V, 48), x == 0, x == 15)

    def spread(ph):
        for k in range(VC * NVC // SC):
            cp(R("Z", 0, 16 * SC, 16), R("meas", PH * SC * k + ph, PH * SC * (k + 1), PH))
            scan(ch("x%d" % ph, k, 16 * SC), R("rmask"), R("Z"), OP.mult, OP.add)

    def prelude(t):
        if t:
            cp(R("KUg"), at(R("KU"), cls(t)))
            ts(R("U"), R("KUg"), 2047, None, OP.bitwise_and)
            cp(R("u16"), R("U"))
            tt(R("EQ"), R("U"), R("P6", 0, I), OP.is_equal)
        else:
            cp(R("U"), at(R("use_i"), cls(t)))
            cp(R("u16"), R("U"))
            tt(R("EQ"), R("U"), lanes("VR", t), OP.is_equal)

    def vpiece(t, k):
        tt(ch("GE", k, 16 * VC), at(MS, ch("u16", k, VC)), ch("x%d" % (t % PH), k, 16 * VC), OP.min)

    def vsum(k):
        mm(ch("P0", k, VC), R("idbig"), ch("EQ", k, VC), True, False)
        for j in range(16):
            mm(ch("P0", k, VC), sk("selm", j), R("GE", 16 * VC * k + j, 16 * VC * (k + 1), 16), False, j == 15)

    def apiece(t, part):
        n = VC * NVC

        def sub(q):
            b = "P3" if q % 2 else "P6"
            for j in range(4):
                mm(ch(b, j, SC), R("idb"), R("meas", PH * n + t % PH, V, PH), True, False)
                mm(ch(b, j, SC), R("idn"), R("GM", 4 * q + j, 16 * SC, 16), False, True)
            act(ch("RA", q, 4 * SC), R(b), AF.Relu)

        def add(q):
            for k in range(4 * q, 4 * q + 4):
                mm(R("P4", n, I), sk("selq", k), ch("RA", k, SC), False, k == 15)

        if part == 0:
            act(R("GM"), at(MS, R("u16", n, I)))
        elif part < 3:
            sub(part - 1)
        elif part == 3:
            mm(R("P4", n, I), R("idbig"), R("EQ", n, I), True, False)
            add(0)
            sub(2)
        elif part == 4:
            add(1)
            sub(3)
        else:
            add(2)
            add(3)

    def winners(keys, kt, ks, n, p2):
        tr(kt, keys)
        scan(ks, R("amask", 0, n), kt, OP.max, OP.min)
        for y in range(2):
            for h in range(2):
                mm(R("P2", p2 + y, p2 + n // 16, 2), ch("swp", 2 * h + y, 128), R(ks[0], 15 + 16 * h, n, 32), h == 0, h == 1)

    def numbers(lst, li, p2, n):
        cp(R(li, 0, n), R("P2", p2, p2 + n))
        ts(R(li, 0, n), R(li, 0, n), 2047, None, OP.bitwise_and)
        cp(R(lst, 0, n), R(li, 0, n))

    def keys(t):
        if t == 0:
            cp(R("KUg"), at(R("KU"), cls(t)))
        n = VC * NVC
        tt(R("KEY", 0, n), R("P0", 0, n), R("KUg", 0, n), OP.add)
        tt(R("KEY", n, I), R("P4", n, I), R("KUg", n, I), OP.add)
        winners(R("KEY"), R("KT"), R("KS"), I, 0)

    def models():
        numbers("m16", "mi", 0, 24)

    def search(t):
        n = {"v": 0, "w": 0}

        def step(z):
            if z == "b":
                prelude(t)
            elif z == "v":
                vpiece(t, n["v"])
            elif z == "w":
                vsum(n["w"])
            elif z in "cdefhi":
                apiece(t, "cdefhi".index(z))
            elif z == "s":
                spread(1)
                spread(2)
            elif z == "p":
                keys(t)
            elif z == "q":
                models()
            if z in n:
                n[z] += 1
        return step

    def gd(k):
        act(ch("GD", k, 16 * CH), at(MO, ch("d16", k, CH)))

    cp(lanes("Bf", 0), lanes("bas_i", 0))
    cp(R("use16"), R("use_i"))
    for ph in (1, 2):
        cp(lanes("Bf", ph), lanes("bas_i", ph))
    ts(R("selp"), R("sel1"), 2048.0, None, OP.mult)
    for k in range(2):
        act(R("SD" if k == 0 else "SE", 0, 4096), at(MS, ch("use16", k, 256)))
    ts(R("pi", 0, 1), R("pi", 0, 1), 15, None, OP.bitwise_and)
    cp(R("pm", 0, 1), R("pi", 0, 1))
    ts(R("pw", 0, 1), R("pm", 0, 1), 1.0, None, OP.add)
    ts(R("pw", 1, 2), R("pm", 0, 1), 8.0, None, OP.mult)
    ts(R("cb", 0, 6), R("cb", 0, 6), col("pm"), 0.5, OP.subtract, OP.subtract)
    ts(R("selz"), R("sel1"), col("pw"), None, OP.mult)
    ts(R("i8"), R("i8"), col("pw", 1), None, OP.add)
    spread(0)
    class_rows(0)
    classes([0, 3], 0)
    ts(R("selm"), R("sel1"), -4096.0, None, OP.mult)
    ts(R("idbig"), R("idb"), BIG, None, OP.mult)
    ts(R("idn"), R("idb"), -1.0, None, OP.mult)
    ts(R("selq"), R("sel1"), 4096.0, None, OP.mult)
    ts(R("blkK"), R("blk"), 2048.0, None, OP.mult)
    for k in range(2):
        mm(R("P5" if k == 0 else "P7", 0, I), R("blkK"), ch("meas", k, I), True, True)
    s0 = search(0)
    s0("b")
    cp(R("d16"), lanes("der_i", 0))
    for k in range(2):
        for j in range(16):
            mm(ch("P1", k, 256), sk("selp", j), R("SD" if k == 0 else "SE", j, 4096, 16), j == 0, j == 15)
    for z in FIRST:
        if z == "p":
            tt(R("NEQ"), R("bas_i"), R("der_i"), OP.not_equal)
            for k in range(2):
                for y in range(2):
                    o = R("KLX", I * k + y, I * k + I, 2)
                    tt(o, R("P5" if k == 0 else "P7", 1 - y, I, 2), o, OP.add)
            tt(R("KU"), R("P1"), R("use_i"), OP.add)
            ts(R("tri"), R("tri"), 8192.0, None, OP.mult)
        s0(z)
        for k in {"e": [0], "h": [1, 2, 3]}.get(z, []):
            gd(k)
        if z == "p":
            for k in range(3):
                p = R("P%d" % (4 + k), 0, I)
                mm(p, R("tri"), ch("NEQ", k, I), True, False)
                mm(p, R("cst"), R("oneb"), False, True)
    mm(R("P7", 0, I), R("blkK"), R("meas", 2 * I, V), True, True)
    class_rows(1)
    class_rows(2)
    for ph in range(PH):
        for x in range(16):
            mm(R("P2", 72 + 24 * ph, 96 + 24 * ph), sk("selz", x), R("meas", 3 * x + ph, V, 48), x == 0, x == 15)
    for k in range(3):
        tt(ch("W", k, I), R("P%d" % (4 + k), 0, I), ch("der_i", k, I), OP.add)
    send(topo, core, asker[0], "qm0", MS, "rm0")
    send(topo, core, asker[0], "qk0", R("KU"), "rk0")
    send(topo, core, asker[0], "qw0", R("W"), "rw0")
    for t in range(1, RO):
        send(topo, core, asker[t], "qm%d" % t, MS, "rm%d" % t)

    def rest1():
        ts(R("blkn"), R("blk"), -1.0, None, OP.mult)
        ts(R("blk2"), R("blk"), 2.0, None, OP.mult)
        ts(R("blk2n"), R("blk"), -2.0, None, OP.mult)
        ts(R("dg"), R("dgf"), col("pm"), None, OP.is_equal)
        cp(R("Dv"), R("der_i"))

    def rest2():
        for y in range(2):
            o = R("KLX", 2 * I + y, V, 2)
            tt(o, R("P7", 1 - y, I, 2), o, OP.add)
        classes([1], 1)
        classes([2], 2)
        for t in range(RO):
            ts(ch("zi", t, 24), ch("P2", 3 + t % PH, 24), float(t), None, OP.add)
        ts(R("zi"), R("zi"), 7, None, OP.bitwise_and)
        tt(R("i8"), R("i8"), R("zi"), OP.add)
        cp(R("zof"), R("i8"))

    def ge(lo, hi, vec):
        o, w = R("GE", 768 * lo, 768 * hi), at(MO, R("e16", 48 * lo, 48 * hi))
        if vec:
            cp(o, w)
        else:
            act(o, w)

    def sd(k):
        scan(ch("SD", k, 16 * CH), R("rmask", 0, 16 * CH), ch("GD", k, 16 * CH), OP.mult, OP.max)

    def se(lo, hi):
        scan(R("SE", 768 * lo, 768 * hi), R("rmask", 0, 768 * (hi - lo)), R("GE", 768 * lo, 768 * hi), OP.mult, OP.max)

    def dist(t):
        ph = t % PH
        lm = lanes("meas", ph)
        half = R("P4", 0, I)
        if t:
            gd(0)
            change(t - 1)
            for k in range(1, 4):
                gd(k)
        ea = R("Ea", 0, I)
        tt(ea, at(R("W"), R("m16")), lanes("Bf", ph), OP.max)
        ts(ea, ea, 4095, None, OP.bitwise_and)
        cp(R("e16"), ea)
        va = [(a, min(a + 2, EV[t])) for a in range(0, EV[t], 2)]
        aa = [(a, min(a + 2, 8)) for a in range(EV[t], 8, 2)]
        act(R("P6", 0, I), lm)
        for a in aa:
            ge(a[0], a[1], False)
        for k, a in enumerate(va):
            ge(a[0], a[1], True)
            sd(k)
        if t == 0:
            rest1()
        for k in range(len(va), 4):
            sd(k)
        for a in va:
            se(a[0], a[1])
        od, oe = R("SD", 15, W16, 16), R("SE", 15, W16, 16)
        tt(R("MD"), od, R("P6", 0, I), OP.min)
        mm(R("P0", 0, I), R("blk"), od, True, False)
        mm(R("P0", 0, I), R("blk2n"), R("MD"), False, True)
        mm(half, R("blkn"), od, True, False)
        mm(half, R("blk2"), R("MD"), False, False)
        for a in aa:
            se(a[0], a[1])
        if t == 0:
            rest2()
        kd, ku = R("P3", 0, I), R("KU", 37 * t, 37 * t + I)
        act(R("KN"), at(R("KLX"), R("m16")))
        act(kd, R("KN"))
        tt(R("ME"), oe, R("P6", 0, I), OP.min)
        mm(half, R("blk"), oe, False, False)
        mm(half, R("blk2n"), R("ME"), False, True)
        tt(kd, kd, ku, OP.subtract)
        act(R("KQ", 0, I), at(R("qk%d" % t), cls(t)))
        act(R("thr", 0, I), R("P0", 0, I), AF.Identity, bias=col("nm"))
        if t + 1 < RO:
            act(R("P6", 0, I), lanes("VR", (t + 1) % PH))
        ts(R("non", 0, I), half, col("nm"), None, OP.is_ge)
        scan(R("cum"), R("non"), R("c128"), OP.add, OP.min)
        for n in range(6):
            act(R("junk"), R("cum"), AF.Sign, bias=col("cb", n), accum=col("acc", n))
        ts(R("got", 0, I), half, col("nm"), None, OP.is_lt)
        tt(kd, kd, R("dg", t, t + I), OP.mult)
        tt(kd, kd, R("got", 0, I), OP.mult)
        tt(ku, kd, ku, OP.add)
        if t + 1 < RO:
            send(topo, core, asker[t + 1], "qk%d" % (t + 1), R("KU"), "rk%d" % (t + 1))

    def ask(t):
        ph = t % PH
        s6, v6 = R("s16", 0, 6), R("sv16", 0, 6)
        zs = R("Z", 0, 16 * CAP, 16)
        ts(s6, R("acc", 0, 6), -0.5, IX / 2.0, OP.mult, OP.add)
        ts(v6, R("acc", 0, 6), -1.5, PH * IX / 2.0 + ph, OP.mult, OP.add)
        cp(R("KQs"), at(R("KQ"), s6))
        ts(R("uq"), R("KQs"), 2047, None, OP.bitwise_and)
        cp(R("uq16"), R("uq"))
        act(zs, at(R("meas"), v6))
        act(R("Bs"), at(R("Bf"), v6))
        act(R("ths"), at(R("thr"), s6))
        scan(R("RQ"), R("rmask", 0, 16 * CAP), R("Z", 0, 16 * CAP), OP.mult, OP.add)
        yield
        act(R("old"), at(MO, zof(t)))
        act(R("P5", 0, I), lanes("Dv", ph))
        for k in range(2):
            tt(ch("GQ", k, 768), at(R("qm%d" % t), ch("uq16", k, 48)), ch("RQ", k, 768), OP.min)
        for j in range(16):
            mm(R("P1", 0, CAP), sk("selm", j), R("GQ", j, 16 * CAP, 16), j == 0, j == 15)
        yield
        tt(R("KEY2"), R("P1", 0, CAP), R("KQs"), OP.add)
        winners(R("KEY2"), R("KT2"), R("KS2"), CAP, 32)
        yield
        numbers("n16", "ni", 32, 6)
        tt(R("E2"), at(R("qw%d" % t), R("n16", 0, 6)), R("Bs"), OP.max)
        ts(R("E2"), R("E2"), 4095, None, OP.bitwise_and)
        cp(R("e216"), R("E2"))
        for k in range(2):
            act(ch("GQ", k, 768), at(MO, ch("e216", k, 48)))
        mm(R("P7", 0, I), R("idb"), lanes("meas", ph), True, False)
        mm(R("P7", 0, I), R("idn"), R("old"), False, True)
        cp(at(R("Ea"), s6), R("E2"))
        if t + 1 < RO:
            cp(R("d16"), lanes("Dv", (t + 1) % PH))
        yield
        for k in range(2):
            scan(ch("S2", k, 768), R("rmask", 0, 768), ch("GQ", k, 768), OP.mult, OP.max)
        tt(R("MM2"), R("S2", 15, 16 * CAP, 16), zs, OP.min)
        mm(R("P1", 0, CAP), R("blk"), R("S2", 15, 16 * CAP, 16), True, False)
        mm(R("P1", 0, CAP), R("blk2n"), R("MM2"), False, True)
        yield
        tt(R("ad2"), R("P1", 0, CAP), R("ths"), OP.is_lt)
        cp(at(R("got"), s6), R("ad2"))
        tt(R("gx"), R("P7", 0, I), R("got", 0, I), OP.mult)
        tt(at(MO, zof(t)), R("old"), R("gx"), OP.add)
        yield

    def change(t):
        ph = t % PH
        last = t + 1 == RO
        d, e = lanes("Dv", ph), R("P5", 0, I)
        if not last:
            keys(t + 1)
        tt(e, e, R("Ea", 0, I), OP.subtract)
        tt(e, e, R("got", 0, I), OP.mult)
        tt(d if last else e, d, e, OP.subtract)
        if last:
            return
        tt(R("NEQ", 0, I), e, lanes("Bf", ph), OP.not_equal)
        cp(d, e)
        models()
        act(R("junk", 0, I), R("got", 0, I), accum=col("cnt"))
        mm(R("P4", 0, I), R("tri"), R("NEQ", 0, I), True, False)
        mm(R("P4", 0, I), R("cst"), R("oneb"), False, True)
        mm(R("P2", 40, 41), R("oall"), col("cnt"), True, True)
        tt(lanes("W", ph), R("P4", 0, I), d, OP.add)
        cp(R("nmi", 0, 1), R("P2", 40, 41))
        ts(R("nmi", 0, 1), R("nmi", 0, 1), 127, None, OP.bitwise_and)
        ts(R("nm", 0, 1), R("nmi", 0, 1), -1.0, None, OP.mult)
        send(topo, core, asker[t + 1], "qw%d" % (t + 1), R("W"), "rw%d" % (t + 1))

    for t in range(RO):
        dist(t)
        a = ask(t)
        if t + 1 < RO:
            s = search(t + 1)
            for z in ORDER:
                if z == "a":
                    next(a)
                else:
                    s(z)
    cp(R("use_i"), R("KU"))
    ts(R("use_i"), R("use_i"), 2047, None, OP.bitwise_and)
    cp(R("KU"), R("use_i"))
    dma("s", T.yu[:], R("KU"))
    for _ in a:
        pass
    dma("a", T.ym[:], MO)
    change(RO - 1)
    dma("s", T.yd[:], R("Dv"))
    F["finish"]()
